import numpy as np, ml_dtypes
CORES = [35,38,43,46]
N = 4
BF = ml_dtypes.bfloat16
def gentries(a):
    return np.ascontiguousarray(a.reshape(8, 16, -1).transpose(0, 2, 1)).reshape(8, -1)
def gtable(e):
    e = np.asarray(e); return np.ascontiguousarray(e.reshape(8, -1, 16).transpose(0, 2, 1)).reshape(128, -1).astype(np.int32)
def f(rng, *shape):
    return (rng.standard_normal(shape, dtype=np.float32) * np.exp2(rng.integers(-2, 3, shape[:-1] + (1,)))).astype(BF)
def wide(rng, *shape):
    v = f(rng, *shape).astype(np.float32); k = shape[:-2] + (1, shape[-1])
    return (v * np.exp2(rng.integers(-6, 7, k)) * (rng.random(k) > 0.0625)).astype(BF)
LV, M, S = 3, 1024, 64
R, A = LV * M, (LV - 1) * (N - 1) * S
W, K = R + A, 4 * M * (LV - 1)
LEV4 = np.repeat(np.concatenate([np.arange(R) // M, np.arange(A) // ((N - 1) * S)]), 4)
OWN4 = np.repeat(np.arange(W) < R, 4).astype(np.float64)
def draw_ent(rng, pri, tidy):
    e = np.zeros((8, LV - 1, 4, M), np.int64)
    for g in range(8):
        free = np.ones(4 * W, bool)
        for l in range(1, LV):
            c = np.flatnonzero(free & (LEV4 < l)); c = c[np.argsort(pri[c] + rng.random(len(c)))[:4 * M]]; free[c] = False
            e[g, l - 1] = np.sort(c).reshape(M, 4)[rng.permutation(M)].T if tidy else rng.permutation(c).reshape(4, M)
    return gtable(e.reshape(8, -1))
def draw_sl(rng, same):
    s = np.zeros((8, LV - 1, N - 1, S), np.int64)
    for g in range(8):
        for l in range(LV - 1):
            if same:
                u = np.concatenate([[0, M - 1], 1 + rng.permutation(M - 2)[:S - 2]]); v = [rng.permutation(u) for d in range(N - 1)]
            else:
                v = [rng.permutation(M)[:S] for d in range(N - 1)]
            s[g, l] = l * M + np.stack(v)
    return gtable(s.reshape(8, -1))
def draw(rng, pri, tidy, same):
    return {"b": f(rng, N, 128, R), "val": ((rng.random((N, 8, K)) - 0.5) * 0.5).astype(BF),
            "ent": np.stack([draw_ent(rng, pri[r], tidy[r]) for r in range(N)]), "sl": np.stack([draw_sl(rng, same) for r in range(N)])}
def setup_inputs(rng):
    return draw(rng, [0 * OWN4] * N, [False] * N, False)
def setup_inputs_same(rng):
    return draw(rng, [OWN4] * N, [False] * N, True)
def setup_inputs_old(rng):
    return draw(rng, [LEV4.astype(np.float64)] * N, [False] * N, False)
def setup_inputs_mixed(rng):
    o = int(rng.integers(0, 2))
    return draw(rng, [1 - OWN4 if (r + o) % 2 else OWN4 for r in range(N)], [(r + o) % 2 == 1 for r in range(N)], False)
def setup_inputs_strong(rng):
    d = setup_inputs(rng); d["val"] = np.where(rng.random((N, 8, K)) < 0.9, -0.25, 0.25).astype(BF); return d
def setup_inputs_spread(rng):
    d = setup_inputs(rng); d["b"] = wide(rng, N, 128, R)
    d["val"] = (d["val"].astype(np.float32) * np.exp2(-rng.integers(0, 7, (N, 8, K))) * (rng.random((N, 8, K)) > 0.0625)).astype(BF); return d
def check_inputs(d):
    bad = []
    if not np.isfinite(d["b"].astype(np.float32)).all(): bad.append("b finite")
    if not (np.abs(d["val"].astype(np.float32)) <= 0.25).all(): bad.append("size of val")
    lv = np.arange(LV - 1)
    for r in range(N):
        e = gentries(d["ent"][r]).astype(np.int64); s = gentries(d["sl"][r]).astype(np.int64).reshape(8, LV - 1, N - 1, S)
        if (e < 0).any() or (e >= 4 * W).any(): bad.append("ent range")
        elif (LEV4[e].reshape(8, LV - 1, 4 * M) > lv[:, None]).any(): bad.append("ent level")
        if (np.diff(np.sort(e, axis=1), axis=1) == 0).any(): bad.append("ent differ")
        if (s // M != lv[:, None, None]).any(): bad.append("sl level")
        if (np.diff(np.sort(s, axis=3), axis=3) == 0).any(): bad.append("sl differ")
    return sorted(set(bad))
def reference(b, val, ent, sl):
    en = np.stack([gentries(ent[r]) for r in range(N)]).astype(np.int64).reshape(N, 8, LV - 1, 4, M); place = en // 4
    se = np.stack([gentries(sl[r]) for r in range(N)]).astype(np.int64).reshape(N, 8, LV - 1, N - 1, S)
    v = val.astype(np.float64).reshape(N, 8, LV - 1, 4, M)
    w = np.zeros((N, 8, 16, W), np.float64); w[..., :R] = b.astype(np.float64).reshape(N, 8, 16, R)
    for l in range(LV):
        for r in range(N):
            for g in range(8):
                if l > 0: w[r, g, :, l * M:(l + 1) * M] -= np.sum(v[r, g, l - 1] * w[r, g][:, place[r, g, l - 1]], axis=1)
                if l < LV - 1:
                    for d in range(N - 1):
                        m = R + (l * (N - 1) + d) * S
                        w[(r + 1 + d) % N, g, :, m:m + S] = w[r, g][:, se[r, g, l, d]]
    z = np.zeros((N, 8, 16, R), np.float64); bk = np.zeros((N, 8, 16, 4 * W), np.float64)
    for l in range(LV - 1, -1, -1):
        for r in range(N):
            for g in range(8):
                x = w[r, g, :, l * M:(l + 1) * M] - np.sum(bk[r, g, :, 4 * l * M:4 * (l + 1) * M].reshape(16, M, 4), axis=2)
                if l < LV - 1:
                    for d in range(N - 1):
                        m = R + (l * (N - 1) + d) * S
                        x[:, se[r, g, l, d] - l * M] -= np.sum(bk[(r + 1 + d) % N, g, :, 4 * m:4 * (m + S)].reshape(16, S, 4), axis=2)
                z[r, g, :, l * M:(l + 1) * M] = x
                if l > 0: bk[r, g][:, en[r, g, l - 1]] = v[r, g, l - 1] * x[:, None, :]
    return {"z": z.reshape(N, 128, R).astype(np.float32)}

from concourse.bass import DstId, RemoteDMATransfer
from concourse.mybir import AluOpType, ActivationFunctionType

N = 4
M = 1024
S = 64
GH = 3 * S
K2, K1 = 216, 76
PAD = 32
E = 4096

NPE = 5
SHARE = 40
ACT0 = [(3, 0), (3, 1), (2, 0), (2, 1), (1, 1)]
ACT1 = [(3, 0), (3, 1), (2, 0), (2, 1)]
CUT = 192
CH2 = [0, 48, 128, 256]

SCRATCH = {
    "slt": ("sbuf", [128, 24], "int32"),
    "slu": ("sbuf", [128, 24], "uint16"),
    "et": ("sbuf", [128, 512], "int32"),
    "ti": ("sbuf", [128, 8 * 256], "int32"),
    "pos2": ("sbuf", [128, 256], "uint16"),
    "pos1": ("sbuf", [128, 256], "uint16"),
    "pl2": ("sbuf", [128, 256], "uint16"),
    "pl1": ("sbuf", [128, 256], "uint16"),
    "bw0": ("sbuf", [128, M + GH], "bfloat16"),
    "b12": ("sbuf", [128, 2 * M], "bfloat16"),
    "w": ("sbuf", [128, 3 * M + 2 * GH], "float32"),
    "neg": ("sbuf", [128, 4 * K1], "float32"),
    "cst": ("sbuf", [128, 128], "float32"),
    "cstb": ("sbuf", [128, 128], "bfloat16"),
    "nI32": ("sbuf", [128, 128], "float32"),
    "pIb": ("sbuf", [128, 128], "bfloat16"),
    "nsel": ("sbuf", [128, 128], "bfloat16"),
    "val8": ("sbuf", [128, 2 * E], "bfloat16"),
    "src": ("sbuf", [128, E], "float32"),
    "win2": ("sbuf", [128, 64 * K2], "float32"),
    "win1": ("sbuf", [128, 64 * K1], "float32"),
    "ext2": ("sbuf", [128, 4, K2], "float32"),
    "ext1": ("sbuf", [128, 4 * K1], "float32"),
    "i1o": ("sbuf", [128, 4, 64], "uint16"),
    "i1g": ("sbuf", [128, 4, 12], "uint16"),
    "i0": ("sbuf", [128, 4 * K1], "uint16"),
    "valb": ("sbuf", [128, 2 * E], "bfloat16"),
    "P": ("sbuf", [128, PAD + 2 * E], "float32"),
    "A": ("sbuf", [128, 3 * M], "float32"),
    "y2": ("sbuf", [128, M], "float32"),
    "z1": ("sbuf", [128, M], "float32"),
    "za": ("sbuf", [128, M], "float32"),
    "z0": ("sbuf", [128, M], "float32"),
    "snd0": ("sbuf", [128, GH], "bfloat16"),
    "snd1": ("sbuf", [128, GH], "float32"),
    "gs1": ("sbuf", [128, GH], "float32"),
    "gs0": ("sbuf", [128, GH], "float32"),
    "rc1": ("sbuf", [128, GH], "float32"),
    "rc0": ("sbuf", [128, GH], "float32"),
    "tmp": ("sbuf", [128, 2 * GH], "float32"),
    "acc": ("psum", [128, M], "float32"),
    "vA": ("psum", [128, M], "float32"),
    "vB": ("psum", [128, M], "float32"),
    "vC": ("psum", [128, M], "float32"),
}
SEMAPHORES = ["cv", "ca", "cp", "cg", "lsl", "lb0", "lb1", "lb2", "le", "lv1", "lv8", "lv2", "fl1", "fl2",
              "ex1", "ex2", "gd0", "st", "arr0", "arr1", "arr2", "arr3", "sent"]

ADD, SUB, MUL = AluOpType.add, AluOpType.subtract, AluOpType.mult
AND, SHR = AluOpType.bitwise_and, AluOpType.logical_shift_right


def engine_masks(topo, core, peers):
    order = sorted(peers, key=lambda c: len(topo.engines(core, c)))
    fewest = len(topo.engines(core, order[0]))
    tight = [c for c in order if len(topo.engines(core, c)) == fewest]
    each = 1
    while 2 * each * len(tight) <= fewest:
        each *= 2
    taken, masks = set(), {}
    for c in order:
        mine = [e for e in topo.engines(core, c) if e not in taken][:each]
        taken.update(mine)
        masks[c] = sum(1 << e for e in mine)
    return masks


def rank_program(g, core, T, topo):
    rank = T.rank_of(core)
    if rank is None:
        return
    cores = list(T.cores)
    others = [c for c in cores if c != core]
    masks = engine_masks(topo, core, others)
    n_in = sum(bin(engine_masks(topo, c, [o for o in cores if o != c])[core]).count("1") for c in others)
    n_out = sum(bin(m).count("1") for m in masks.values())

    Q = {"g": g, "v": g.vector, "a": g.scalar, "p": g.tensor, "s": g.sync}
    total, seen = {}, {}

    def wait(q, *toks):
        for sem, n in toks:
            if seen.get((q, sem), 0) < n:
                Q[q].wait_ge(T.sem[sem], n)
                seen[(q, sem)] = n

    def mark(inst, sem, n):
        inst.then_inc(T.sem[sem], n)
        total[sem] = total.get(sem, 0) + n
        return (sem, total[sem])

    def done(q, inst):
        return mark(inst, "c" + q, 1)

    def dma(q, sem, out, in_, *deps):
        wait(q, *deps)
        return mark(Q[q].dma_start(out, in_), sem, 16)

    V, ACT, PE = g.vector, g.scalar, g.tensor

    def v_copy(out, in_, *deps):
        wait("v", *deps)
        return done("v", V.tensor_copy(out, in_))

    def v_tt(out, a, b, op, *deps):
        wait("v", *deps)
        return done("v", V.tensor_tensor(out, a, b, op))

    def v_ts(out, a, s1, s2, op0, op1, *deps):
        wait("v", *deps)
        if s2 is None:
            return done("v", V.tensor_scalar(out, a, s1, None, op0))
        return done("v", V.tensor_scalar(out, a, s1, s2, op0, op1))

    def mm(out, lhsT, rhs, start, stop, *deps):
        wait("p", *deps)
        return done("p", PE.matmul(out, lhsT, rhs, start, stop))

    def exchange(sem, src, dst_of, step, *deps):
        wait("g", *deps)
        transfers = []
        for d in range(N - 1):
            c = cores[(rank + step * (1 + d)) % N]
            rid, pid, _ = topo.addr(c)
            transfers.append(RemoteDMATransfer(dst_ids=[DstId(rid=rid, pnc=pid)], dma_engine_mask=masks[c],
                                               remote_sem=T.sem[sem], src=src[:, d * S:(d + 1) * S], dst=dst_of(d)))
        g.remote_dma_fused(transfers, local_sem=T.sem.sent)
        total["sent"] = total.get("sent", 0) + n_out
        total[sem] = n_in
        return (sem, n_in)

    def half(buf, h, base=0):
        return buf[:, base + 512 * h: base + 512 * (h + 1)]

    t_cstb = done("v", V.memset(T.cstb[0:8, :], -1.0))
    t_cst = done("v", V.memset(T.cst[:], -1.0))
    t_zero = done("v", V.memset(T.w[:, 2 * M:3 * M], 0.0))
    t_neg = done("v", V.memset(T.neg[:], -float(E)))
    t_pad = done("v", V.memset(T.P[:, 0:PAD], 0.0))

    t_b0 = dma("s", "lb0", T.bw0[:, 0:M], T.b[:, 0:M])
    t_v8 = dma("a", "lv1", T.val8[0:8, 0:E], T.val[:, 0:E])
    t_sl = dma("a", "lsl", T.slt[:], T.sl[:])
    t_e = dma("s", "le", T.et[:], T.ent[:])
    t_f2 = dma("s", "fl2", T.win2[0::16, :], T.w[:, 2 * M:2 * M + 4 * K2], t_zero)
    t_b1 = dma("s", "lb1", T.b12[:, 0:M], T.b[:, M:2 * M])

    wait("g", t_cstb)
    t_sel = done("g", g.affine_select(T.nsel[0:8, :], T.cstb[0:8, :], [[1, 8], [0, 16]], AluOpType.is_equal,
                                      0.0, 0, -1))
    wait("g", t_cst)
    t_nI = done("g", g.affine_select(T.nI32[:], T.cst[:], [[-1, 128]], AluOpType.is_equal, 0.0, 0, 1))
    wait("a", t_nI)
    t_pIb = done("a", ACT.activation(T.pIb[:], T.nI32[:], ActivationFunctionType.Copy, scale=-1.0))

    def factors(bank, level, e, *deps):
        for h in range(2):
            a = E * (level - 1) + M * e + 512 * h
            t = mm(half(bank, h), T.nsel[0:8, :], T.val8[0:8, a:a + 512], True, True, *deps)
        return t

    banks = [T.vA, T.vB, T.vC, T.acc]
    t_v1 = []
    for e in range(4):
        t = factors(banks[e % 3], 1, e, t_v8, t_sel, *t_v1[0:e // 3])
        wait("a", t)
        t_v1.append(done("a", ACT.activation(T.valb[:, M * e:M * (e + 1)], banks[e % 3][:],
                                             ActivationFunctionType.Copy, scale=-1.0)))

    def numbers(i):
        a, b = 16 * CH2[i], 16 * CH2[i + 1]
        return done("g", g.iota(T.src[:, a:b], [[1, b - a]], PAD + a, 0, allow_small_or_imprecise_dtypes=True))

    t_src = [numbers(0)]

    t_s0 = v_copy(T.slu[:, 0:12], T.slt[:, 0:12], t_sl)
    t_s1 = v_ts(T.slu[:, 12:24], T.slt[:, 12:24], float(M), None, SUB, None)
    t = v_copy(T.snd0[:], T.bw0[:, 0:M].indirect(T.slu[:, 0:12]), t_s0, t_b0)
    t_arr0 = exchange("arr0", T.snd0, lambda d: T.bw0[:, M + d * S:M + (d + 1) * S], 1, t)
    t_w0 = dma("g", "gd0", T.w[:, 0:M], T.b[:, 0:M])
    for i in range(1, len(CH2) - 1):
        t_src.append(numbers(i))
    t_f1 = dma("s", "fl1", T.win1[0::16, :], T.neg[:], t_neg, t_arr0)
    t_b2 = dma("s", "lb2", T.b12[:, M:2 * M], T.b[:, 2 * M:3 * M])
    t_v8b = dma("s", "lv8", T.val8[0:8, E:2 * E], T.val[:, E:2 * E])
    for c in range(16):
        t_v2 = dma("s", "lv2", T.valb[c::16, E:2 * E], T.val[:, E:2 * E])

    def tcol(i):
        return T.ti[:, 256 * i:256 * (i + 1)]

    def positions(out, ent, k, wrap, i, *deps):
        ps = T.acc[:, 0:256]
        t0 = v_ts(tcol(i), ent, 63, None, AND, None, *deps)
        if wrap:
            t1 = v_ts(tcol(i + 1), ent, 6, 127, SHR, AND)
        else:
            t1 = v_ts(tcol(i + 1), ent, 6, None, SHR, None)
        t2 = v_ts(ps, tcol(i), float(k), None, MUL, None, t0)
        t3 = v_tt(tcol(i + 2), ps, tcol(i + 1), ADD, t1, t2)
        return v_copy(out, tcol(i + 2), t3)

    t_pos2 = positions(T.pos2[:], T.et[:, 256:512], K2, False, 0, t_e)
    t = v_ts(tcol(6), T.et[:, 0:256], 2, 2 * M - 1, SHR, AND)
    t_pl1 = v_copy(T.pl1[:], tcol(6), t)
    t_pos1 = positions(T.pos1[:], T.et[:, 0:256], K1, True, 3, t_pos2)

    t = None
    for i in range(len(CH2) - 1):
        a, b = CH2[i], CH2[i + 1]
        wait("a", t_pos2, t_f2, t_src[i], *([t] if t else []))
        t = done("a", ACT.activation(T.win2[:, :].indirect(T.pos2[:, a:b]), T.src[:, 16 * a:16 * b],
                                     ActivationFunctionType.Silu))
    t_x2 = dma("s", "ex2", T.ext2[:], T.win2[0::16, :], t)

    PR = PAD + E

    def forward(level, window, places, out, o0, v_deps, p_deps, t_val):
        v0 = E * (level - 1)
        on_pe = [(0, 0), (0, 1), (1, 1), (1, 0), (2, 0), (2, 1)][:NPE]
        for h in range(2):
            mm(half(T.acc, h), T.pIb[:], half(T.b12, h, M * (level - 1)), True, False, *p_deps)
        prod = {}
        for a, b in [(0, 512), (512, M), (M, 2 * M), (2 * M, 3 * M), (3 * M, 4 * M)]:
            t = v_tt(T.P[:, PR + a:PR + b], window.indirect(places[:, a // 16:b // 16]), T.valb[:, v0 + a:v0 + b],
                     MUL, *v_deps, t_val[a // M])
            for x in range(a, b, 512):
                prod[(x // M, x % M // 512)] = t
        last = {}
        for n, (e, h) in enumerate(on_pe):
            stop = all(hh != h for _, hh in on_pe[n + 1:])
            last[h] = mm(half(T.acc, h), T.nI32[:], half(T.P, h, PR + M * e), False, stop, prod[(e, h)])
        fin = []
        for h in (1, 0):
            rest = [e for e in range(4) if (e, h) not in on_pe]
            t = last[h]
            for e in rest[:-1]:
                t = v_tt(half(T.acc, h), half(T.acc, h), half(T.P, h, PR + M * e), SUB, t, prod[(e, h)])
            fin.append(v_tt(half(out, h, o0), half(T.acc, h), half(T.P, h, PR + M * rest[-1]), SUB, t,
                            prod[(rest[-1], h)]))
        return fin[-1]

    t_y1 = forward(1, T.bw0[:, :], T.pl1, T.w, M, [t_pl1, t_arr0], [t_b1, t_pIb, t_nI, t_pos1], t_v1)
    t = v_copy(T.snd1[:], T.w[:, M:2 * M].indirect(T.slu[:, 12:24]), t_y1, t_s1)
    t_arr1 = exchange("arr1", T.snd1, lambda d: T.w[:, 3 * M + GH + d * S:3 * M + GH + (d + 1) * S], 1, t)
    t_fac = [factors(banks[e], 2, e, t_v1[3], t_v8b) for e in range(3)]

    t_w0g = v_copy(T.w[:, 3 * M:3 * M + GH], T.bw0[:, M:M + GH], t_arr0)
    t = v_ts(tcol(7), T.et[:, 256:512], 2, None, SHR, None)
    t_pl2 = v_copy(T.pl2[:], tcol(7), t)
    after = [t_f1, t_pos1, t_src[-1]]
    if SHARE:
        after.append(v_copy(T.win1[:, :].indirect(T.pos1[:, 0:SHARE]), T.src[:, 0:16 * SHARE], *after))

    def invert1(a, b, *deps):
        wait("a", *deps)
        return done("a", ACT.activation(T.win1[:, :].indirect(T.pos1[:, a:b]), T.src[:, 16 * a:16 * b],
                                        ActivationFunctionType.Silu))

    if CUT > SHARE:
        after.append(invert1(SHARE, CUT, *after))
    if CUT == 256:
        t_x1 = dma("a", "ex1", T.ext1[:], T.win1[0::16, :], *after)

    t_y2 = forward(2, T.w[:, :], T.pl2, T.y2, 0, [t_pl2, t_arr1, t_w0, t_w0g, t_y1], [t_b2, t_y1], [t_v2] * 4)
    t_fac.append(factors(T.acc, 2, 3, t_y2))
    dma("s", "st", T.z[:, 2 * M:3 * M], T.y2[:], t_y2)

    def products(base, zz, t_z):
        return [v_tt(T.P[:, base + M * e:base + M * (e + 1)], banks[e][:], zz[:], MUL, t_z, t_fac[e])
                for e in range(4)]

    def ghosts(out, window, lists, *deps):
        t = v_copy(out[:], window.indirect(lists(0)), *deps)
        for s in range(1, 4):
            t = v_tt(out[:], window.indirect(lists(s)), out[:], ADD, t)
        return t

    def own(out, b0, window, lists, skip, *deps):
        t, first = None, True
        for s in range(4):
            hs = [h for h in range(2) if (s, h) not in skip]
            if not hs:
                continue
            a, b = 512 * hs[0], 512 * (hs[-1] + 1)
            t = v_tt(out[:, a:b], window.indirect(lists(s, a // 16, b // 16)),
                     T.w[:, b0 + a:b0 + b] if first else out[:, a:b], ADD, *(deps if first else [t]))
            first = False
        return t

    def adjust(out, h, rc, t, t_arr):
        for d in range(N - 1):
            lst = T.slu[:, 12 * h + 4 * d:12 * h + 4 * (d + 1)]
            tm = T.tmp[:, GH * h + S * d:GH * h + S * (d + 1)]
            t = v_tt(tm, out[:, :].indirect(lst), rc[:, S * d:S * (d + 1)], ADD, t, t_arr)
            t = v_copy(out[:, :].indirect(lst), tm, t)
        return t

    def helped(pieces, win, lists, *deps):
        last = {}
        for n, (s, h) in enumerate(pieces):
            wait("a", *deps)
            piece = half(T.A, h, M * (s - 1))
            t = done("a", ACT.activation(piece, win.indirect(lists(s, 32 * h, 32 * (h + 1))),
                                         ActivationFunctionType.Copy))
            last[h] = mm(half(T.acc, h), T.nI32[:], piece, h not in last, all(hh != h for _, hh in pieces[n + 1:]),
                         t, *deps)
        return last

    t_m2 = products(PAD, T.y2, t_y2)
    t_fac = [factors(banks[e], 1, e, t_m2[e]) for e in range(3)]
    t_a = v_ts(T.i1g[:], T.ext2[:, :, 204:216], 0.25, None, ADD, None, t_x2)
    t_b = v_ts(T.i1o[:], T.ext2[:, :, 64:128], 0.25, None, ADD, None)
    win = T.P[:, 0:PAD + E]
    last = helped(ACT1, win, lambda s, a, b: T.i1o[:, s, a:b], t_b, t_m2[3], t_pad)
    if CUT < 256:
        t_x1 = dma("a", "ex1", T.ext1[:], T.win1[0::16, :], invert1(max(CUT, SHARE), 256, *after))
    t = ghosts(T.gs1, win, lambda s: T.i1g[:, s, :], t_a, t_m2[3], t_pad)
    t_arr2 = exchange("arr2", T.gs1, lambda d: T.rc1[:, d * S:(d + 1) * S], -1, t)
    z1 = T.za if ACT1 else T.z1
    t = own(z1, M, win, lambda s, a, b: T.i1o[:, s, a:b], ACT1, t_b)
    t_z1 = adjust(z1, 1, T.rc1, t, t_arr2)
    if ACT1:
        t_z1 = v_tt(T.z1[:], T.za[:], T.acc[:], SUB, t_z1, last[0], last[1])
    t_fac.append(factors(T.acc, 1, 3, t_z1))
    dma("s", "st", T.z[:, M:2 * M], T.z1[:], t_z1)

    t_m1 = products(PR, T.z1, t_z1)
    mm(T.vA[:, 0:4 * K1], T.nI32[:], T.ext1[:], True, False, t_m1[0], t_x1, t_x2)
    for s in range(4):
        mm(T.vA[:, K1 * s:K1 * s + 64], T.nI32[:], T.ext2[:, s, 0:64], False, False)
        t = mm(T.vA[:, K1 * s + 64:K1 * (s + 1)], T.nI32[:], T.ext2[:, s, 192:204], False, s == 3)
    t_i0 = v_ts(T.i0[:], T.vA[:, 0:4 * K1], -1.0, E + 0.25, MUL, ADD, t)
    win = T.P[:, :]
    last = helped(ACT0, win, lambda s, a, b: T.i0[:, K1 * s + a:K1 * s + b], t_i0, t_m1[3])
    t = ghosts(T.gs0, win, lambda s: T.i0[:, K1 * s + 64:K1 * (s + 1)], t_i0, t_m1[3])
    t_arr3 = exchange("arr3", T.gs0, lambda d: T.rc0[:, d * S:(d + 1) * S], -1, t)
    t = own(T.za, 0, win, lambda s, a, b: T.i0[:, K1 * s + a:K1 * s + b], ACT0, t_i0)
    t = adjust(T.za, 0, T.rc0, t, t_arr3)
    for h in range(2):
        tz = v_tt(half(T.z0, h), half(T.za, h), half(T.acc, h), SUB, t, last[h])
        dma("sa"[h], "st", half(T.z, h), half(T.z0, h), tz)

    wait("g", ("sent", total["sent"]))
    wait("s", *[(s, n) for s, n in total.items() if s not in ("sent", "gd0")])
